import numpy as np
import ml_dtypes


def mxq(x, axis, fmt="e4m3"):
    dtype, down = {"e4m3": (ml_dtypes.float8_e4m3fn, 7), "e5m2": (ml_dtypes.float8_e5m2, 14)}[fmt]
    v = np.moveaxis(np.asarray(x, np.float32).astype(ml_dtypes.bfloat16).astype(np.float64), axis, -1)
    blocks = v.reshape(v.shape[:-1] + (-1, 32))
    amax = np.abs(blocks).max(-1, keepdims=True)
    byte = np.maximum(np.where(amax > 0, np.frexp(amax)[1] - 1 + 127, 0) - down, 1)
    scale = np.exp2(byte - 127.0)
    codes = (blocks / scale).astype(np.float32).astype(dtype).astype(np.float64)
    return np.moveaxis((codes * scale).reshape(v.shape), -1, axis)


WIDE = False


def mx_kscale(k):
    if not WIDE:
        return np.ones(k)
    levels = np.array([10, -10, 5, -5, 0])
    if k % 512:
        return np.exp2(np.random.permutation(np.resize(levels, k // 32))).repeat(32)
    a = np.empty((k // 512, 16))
    for p in range(k // 512):
        a[p, :8] = np.random.permutation(np.resize(levels, 8))
        for g in range(8):
            far = levels[np.abs(levels - a[p, g]) >= 10]
            a[p, g + 8] = far[np.random.randint(len(far))]
    return np.exp2(a.ravel()).repeat(32)


def f64(x):
    return np.asarray(x).astype(np.float64)


def striped(idx):
    return np.tile(idx.reshape(-1, 16).T, (8, 1)).astype(np.uint16)


def unstriped(offs):
    return offs[:16].T.reshape(-1).astype(np.int64)


E2M1 = np.array([0.0, 0.5, 1.0, 1.5, 2.0, 3.0, 4.0, 6.0, -0.0, -0.5, -1.0, -1.5, -2.0, -3.0, -4.0, -6.0])


def pack_weight(w, fmt):
    k, n = w.shape
    w = f64(np.asarray(w, np.float32).astype(ml_dtypes.bfloat16)).reshape(k // 32, 32, n)
    amax = np.abs(w).max(1)
    if fmt == "e4m3":
        byte = np.frexp(amax)[1] - 1 + 127 - 7
    else:
        mant, ex = np.frexp(amax / 6.0)
        byte = np.where(mant > 0.5, ex, ex - 1) + 127
    byte = np.clip(np.where(amax > 0, byte, 1), 1, 254)
    scaled = (w * np.exp2(127.0 - byte)[:, None, :]).reshape(k, n).astype(np.float32)
    by_word = np.ascontiguousarray(scaled.reshape(k // 512, 128, 4, n).transpose(0, 1, 3, 2))
    if fmt == "e4m3":
        words = by_word.astype(ml_dtypes.float8_e4m3fn).view(np.uint8)
    else:
        c = by_word.astype(ml_dtypes.float4_e2m1fn).view(np.uint8) & 0xF
        words = (c[..., 0::2] | (c[..., 1::2] << 4)).reshape(k // 512, 128, 2 * n)
    return np.ascontiguousarray(words), np.ascontiguousarray(byte.astype(np.uint8).reshape(k // 512, 16, n))


def unpack_weight(words, scales, fmt):
    g, _, n = scales.shape
    words = np.ascontiguousarray(words).reshape(g, 128, n, -1)
    if fmt == "e4m3":
        vals = words.view(ml_dtypes.float8_e4m3fn).astype(np.float64)
    else:
        nib = np.empty((g, 128, n, 4), np.uint8)
        nib[..., 0::2] = words & 0xF
        nib[..., 1::2] = words >> 4
        vals = E2M1[nib]
    vals = vals * np.repeat(np.exp2(scales.astype(np.float64) - 127.0), 8, axis=1)[..., None]
    return vals.transpose(0, 1, 3, 2).reshape(g * 512, n)


def gelu(v):
    return 0.5 * v * (1.0 + np.tanh(np.sqrt(2.0 / np.pi) * (v + 0.044715 * v**3)))


def bf(x):
    return np.asarray(x, np.float32).astype(ml_dtypes.bfloat16)


def planes(Y):
    n, m = Y.shape
    b = f64(bf(Y)).reshape(n // 32, 32, m)
    amax = np.abs(b).max(1)
    byte = np.clip(np.where(amax > 0, np.frexp(amax)[1] - 1 + 127 - 7, 1), 1, 254)
    codes = (b * np.exp2(127.0 - byte)[:, None, :]).reshape(n, m).astype(np.float32).astype(ml_dtypes.float8_e4m3fn).view(np.uint8)
    words = codes.reshape(n // 512, 128, 4, m).transpose(0, 1, 3, 2)
    return np.ascontiguousarray(words), np.ascontiguousarray(byte.astype(np.uint8).reshape(n // 512, 16, m))


K, H, N, T, S, T2, P = 1024, 512, 512, 4096, 1024, 2048, 512

def setup_inputs():
    n = np.random.standard_normal
    s = mx_kscale(K)[:, None]
    u = mx_kscale(H)[:, None]
    d = {}
    shape = np.sign(n((K, 1)))
    strength = np.random.uniform(-1.0, 1.0, (1, T))
    d["tab_words"], d["tab_scales"] = pack_weight((0.8 * n((K, T)) + shape * strength) * s, "e4m3")
    d["offs"] = striped(np.random.permutation(T)[:S])
    d["offs2"] = striped(np.random.permutation(T2)[:S])
    d["offs3"] = striped(np.random.permutation(T2)[:P])
    d["w1"] = ((0.18 * n((K, H)) / K ** 0.5 + 1.9 * shape * np.sign(n((1, H))) / K) / s).astype(np.float32)
    d["w2_words"], d["w2_scales"] = pack_weight(0.48 * n((K, H)) / K ** 0.5 / s, "e2m1")
    d["gain"] = (np.exp(0.3 * n(H)) * u[:, 0]).astype(np.float32)
    d["wgs"] = np.exp(0.3 * n((128, S))).astype(np.float32)
    d["page0"] = (0.7 * n((H, T2)) * u).astype(np.float32)
    d["norm"] = (0.5 * n((H, P)) * u).astype(np.float32)
    d["w3"] = (n((H, N)) / H ** 0.5 / u).astype(np.float32)
    return d

def reference(tab_words, tab_scales, offs, offs2, offs3, w1, w2_words, w2_scales, gain, wgs, page0, norm, w3):
    v = unpack_weight(tab_words, tab_scales, "e4m3")[:, unstriped(offs)]
    w2 = unpack_weight(w2_words, w2_scales, "e2m1")
    a = mxq(f64(w1), 0, "e4m3").T @ v
    b = w2.T @ v
    h = f64(gain)[:, None] * (np.sin(a) + np.cos(b))
    page = f64(page0).copy()
    page[:, unstriped(offs2)] = np.tile(f64(wgs), (H // 128, 1)) * h
    x = page[:, unstriped(offs3)] - f64(norm)
    y = np.abs(mxq(f64(w3), 0, "e4m3").T @ mxq(x, 0, "e4m3"))
    words, scales = planes(page)
    return y, page, words, scales

@@ -1,0 +1,324 @@
+import math
+from contextlib import ExitStack
+
+import concourse.mybir as mybir
+from concourse.masks import make_identity
+
+K, H, N, T, S, T2, R = 1024, 512, 512, 4096, 1024, 2048, 512
+FLOPS = 2 * (2 * K * H * S + H * N * R)
+
+F32 = mybir.dt.float32
+BF16 = mybir.dt.bfloat16
+I32 = mybir.dt.int32
+U32 = mybir.dt.uint32
+U16 = mybir.dt.uint16
+U8 = mybir.dt.uint8
+FP8X4 = mybir.dt.float8_e4m3fn_x4
+FP4X4 = mybir.dt.float4_e2m1fn_x4
+ACT = mybir.ActivationFunctionType
+ALU = mybir.AluOpType
+
+P = 128
+PACK = 4
+PASSES = K // (P * PACK)
+JB = S // P
+HALF = S // 2
+QUARTER = S // 4
+CHUNK = 512
+XH = R // 2
+
+
+def tile_list_head_impulse_page_kernel(
+    tc, tab_words, tab_scales, offs, offs2, offs3, w1, w2_words, w2_scales, gain, wgs, page0, norm, w3,
+    out_0, out_1, out_2, out_3,
+):
+    nc = tc.nc
+    with ExitStack() as ctx:
+        keep = ctx.enter_context(tc.tile_pool(name="keep", bufs=1))
+        ring = ctx.enter_context(tc.tile_pool(name="ring", bufs=2))
+        psum = ctx.enter_context(tc.psum_pool(name="psum", bufs=2))
+
+        idx = keep.tile([P, S // 16], U16, name="idx")
+        idx2 = keep.tile([P, S // 16], U16, name="idx2")
+        idx3 = keep.tile([P, R // 16], U16, name="idx3")
+        tab = [keep.tile([P, T], U32, name=f"tab{a}") for a in range(PASSES)]
+        tab_rows = keep.tile([P, T], U8, name="tab_rows")
+        picked_rows = keep.tile([P, S], U8, name="picked_rows")
+        v_scales = keep.tile([P, PASSES, S], U8, name="v_scales", align_bytes=64)
+        v_words = [keep.tile([P, S], U32, name=f"v_words{a}", align_bytes=64) for a in range(PASSES)]
+        w2_codes = keep.tile([P, PASSES, 2 * H], U8, name="w2_codes", align_bytes=64)
+        w2_plane = keep.tile([P, PASSES, H], U8, name="w2_plane", align_bytes=64)
+        w1_codes = keep.tile([P, PASSES, H], U32, name="w1_codes", align_bytes=64)
+        w1_plane = keep.tile([P, PASSES, H], U8, name="w1_plane", align_bytes=64)
+        g = keep.tile([P, PACK], F32, name="g")
+        g_neg = keep.tile([P, PACK], F32, name="g_neg")
+        wg = keep.tile([P, PACK, S], F32, name="wg")
+        page = [keep.tile([P, T2], F32, name=f"page{t}") for t in range(PACK)]
+        norm_sb = keep.tile([P, PACK, R], F32, name="norm_sb")
+        w3_raw = keep.tile([P, PACK, N], F32, name="w3_raw")
+        w3_codes = keep.tile([P, N], U32, name="w3_codes", align_bytes=64)
+        w3_plane = keep.tile([P, N], U8, name="w3_plane", align_bytes=64)
+        ident = keep.tile([P, P], F32, name="ident")
+        clock = keep.tile([P, 16], F32, name="clock")
+        warm = keep.tile([P, 1], F32, name="warm")
+        two_sq = [keep.tile([P, PACK, P], F32, name=f"two_sq{j}") for j in range(JB)]
+        neg_sin = [keep.tile([P, PACK, P], F32, name=f"neg_sin{j}") for j in range(JB)]
+        page_plane = keep.tile([P, T2], U8, name="page_plane", align_bytes=64)
+
+        page_rows = page0.rearrange("(p t) m -> t p m", t=PACK)
+        out_rows = out_1.rearrange("(p t) m -> t p m", t=PACK)
+        wgs_rows = wgs.rearrange("(q t) j -> q t j", t=PACK)
+
+        def load_wg(ts, js):
+            for quad in range(4):
+                nc.sync.dma_start(out=wg[32 * quad : 32 * quad + 32, ts, js], in_=wgs_rows[:, ts, js])
+
+        def load_table(a):
+            nc.sync.dma_start(
+                out=tab[a][:].bitcast(I32), in_=tab_words[a].rearrange("p t i -> p (t i)").bitcast(I32)
+            )
+
+        nc.vector.memset(tab_rows[32:64, :].bitcast(I32), 0)
+        nc.vector.memset(tab_rows[64:128, :].bitcast(I32), 0)
+        nc.vector.memset(w2_plane[:].rearrange("p a t -> p (a t)").bitcast(I32), 0)
+        nc.vector.memset(v_scales[:].rearrange("p a t -> p (a t)").bitcast(I32), 0)
+        make_identity(nc, ident[:])
+
+        nc.sync.dma_start(idx[:], offs)
+        nc.sync.dma_start(
+            out=tab_rows[0:32, :].bitcast(I32), in_=tab_scales.rearrange("a q t -> q a t").bitcast(I32)
+        )
+        load_table(0)
+        nc.sync.dma_start(out=w2_codes[:].bitcast(I32), in_=w2_words.rearrange("a p c -> p a c").bitcast(I32))
+        for quad in range(4):
+            nc.scalar.dma_start(
+                out=w2_plane[32 * quad : 32 * quad + 4, :, :].bitcast(I32),
+                in_=w2_scales[:, 4 * quad : 4 * quad + 4, :].rearrange("a r c -> r a c").bitcast(I32),
+            )
+        w1_raw = {}
+
+        def load_w1(a):
+            for c in range(2):
+                w1_raw[a, c] = ring.tile([P, PACK, H // 2], F32, name=f"w1_raw{a}{c}", tag="four_kib", bufs=4)
+                rows = w1[512 * a : 512 * (a + 1), (H // 2) * c : (H // 2) * (c + 1)]
+                nc.sync.dma_start(out=w1_raw[a, c][:], in_=rows.rearrange("(p i) c -> p i c", i=PACK))
+
+        load_table(1)
+        load_w1(0)
+        load_w1(1)
+        first, second = slice(0, HALF), slice(HALF, S)
+        nc.sync.dma_start(idx2[:], offs2)
+        nc.sync.dma_start(out=g[:], in_=gain.rearrange("(p t) -> p t", t=PACK))
+        nc.sync.dma_start(out=page[0][:], in_=page_rows[0])
+        load_wg(slice(0, 2), slice(0, QUARTER))
+        nc.sync.dma_start(out=page[1][:], in_=page_rows[1])
+        load_wg(slice(0, 2), slice(QUARTER, HALF))
+        nc.sync.dma_start(out=page[2][:], in_=page_rows[2])
+        load_wg(slice(2, 4), first)
+        load_wg(slice(0, 2), second)
+        nc.sync.dma_start(out=w3_raw[:], in_=w3.rearrange("(p i) n -> p i n", i=PACK))
+        load_wg(slice(2, 4), second)
+        nc.sync.dma_start(out=page[3][:], in_=page_rows[3])
+        nc.sync.dma_start(idx3[:], offs3)
+        nc.sync.dma_start(out=norm_sb[:], in_=norm.rearrange("(p t) j -> p t j", t=PACK))
+
+        nc.scalar.activation(warm[:], ident[:, 0:1], ACT.Sin)
+
+        nc.vector.tensor_copy(picked_rows[:], tab_rows[:].indirect(idx[:]))
+        for quad in range(4):
+            nc.scalar.dma_start(
+                out=v_scales[32 * quad : 32 * quad + 4, :, :].bitcast(I32),
+                in_=picked_rows[8 * quad : 8 * quad + 8, :].bitcast(I32),
+            )
+        nc.vector.tensor_copy(v_words[0][:], tab[0][:].indirect(idx[:]))
+
+        def pick_second_pass(half):
+            cols = slice(HALF * half, HALF * (half + 1))
+            nc.vector.tensor_copy(
+                v_words[1][:, cols], tab[1][:].indirect(idx[:, (HALF // 16) * half : (HALF // 16) * (half + 1)])
+            )
+
+        def quantise_w1(a, c):
+            grouped = ring.tile([P, H // 2, PACK], BF16, name="w1_grouped", tag="w1_grouped", align_bytes=64)
+            rows = w1_raw[a, c][:].rearrange("p i c -> p c i")
+            if (a, c) == (0, 0):
+                nc.scalar.copy(out=grouped[:], in_=rows)
+            else:
+                nc.vector.tensor_copy(out=grouped[:], in_=rows)
+            cols = slice((H // 2) * c, (H // 2) * (c + 1))
+            nc.vector.quantize_mx(
+                out=w1_codes[:, a, cols].bitcast(FP8X4),
+                scales=w1_plane[:, a, cols],
+                in_=grouped[:].rearrange("p c i -> p (c i)"),
+            )
+
+        pick_second_pass(0)
+        pick_second_pass(1)
+        for a in range(PASSES):
+            for c in range(2):
+                quantise_w1(a, c)
+        nc.vector.tensor_scalar(g_neg[:], g[:], -1.0, None, ALU.mult)
+
+        def table_pass(bank, j, a, codes, plane):
+            cols = slice(P * j, P * (j + 1))
+            nc.tensor.matmul_mx(
+                out=bank[:],
+                lhsT=v_words[a][:, cols].bitcast(FP8X4),
+                lhsT_scale=v_scales[:, a, cols],
+                rhs=codes,
+                rhs_scale=plane,
+                start=(a == 0),
+                stop=(a == PASSES - 1),
+            )
+
+        def cosine_part(j):
+            bank = psum.tile([P, H], F32, name="b_bank", tag="sum" if j < 4 else "a", bufs=4)
+            for a in range(PASSES):
+                table_pass(bank, j, a, w2_codes[:, a, :].bitcast(FP4X4), w2_plane[:, a, :])
+            half_sin = ring.tile([P, PACK, P], F32, name="half_sin")
+            nc.scalar.activation(half_sin[:], bank[:].rearrange("p (q t) -> p t q", t=PACK), ACT.Sin, scale=0.5)
+            nc.scalar.activation(two_sq[j][:], half_sin[:], ACT.Square, scale=math.sqrt(2.0))
+
+        def sine_part(js):
+            banks = [psum.tile([P, H], F32, name=f"a_bank{j}", tag="a", bufs=4) for j in js]
+            for a in range(PASSES):
+                for bank, j in zip(banks, js):
+                    table_pass(bank, j, a, w1_codes[:, a, :].bitcast(FP8X4), w1_plane[:, a, :])
+            for bank, j in zip(banks, js):
+                nc.scalar.activation(
+                    neg_sin[j][:], bank[:].rearrange("p (q t) -> p t q", t=PACK), ACT.Sin, scale=-1.0
+                )
+
+        def put(t, j0, j1, tag="h", bufs=3):
+            width = P * (j1 - j0)
+            bank = psum.tile([P, width], F32, name="sum_bank", tag="sum", bufs=4)
+            for j in range(j0, j1):
+                cols = slice(P * (j - j0), P * (j - j0 + 1))
+                nc.tensor.matmul(
+                    bank[:, cols], two_sq[j][:, t, :], ident[:], start=True, stop=False, is_transpose=True
+                )
+                nc.tensor.matmul(
+                    bank[:, cols], neg_sin[j][:, t, :], ident[:], start=False, stop=True, is_transpose=True
+                )
+            h = ring.tile([P, width], F32, name="h", tag=tag, bufs=bufs)
+            nc.scalar.activation(h[:], bank[:], ACT.Identity, bias=g[:, t : t + 1], scale=g_neg[:, t : t + 1])
+            if t == 0 and j0 == 0:
+                nc.gpsimd.tensor_copy(clock[:, 0:1], h[:, 0:1])
+            places = idx2[:, (P // 16) * j0 : (P // 16) * j1]
+            nc.vector.tensor_tensor(page[t][:].indirect(places), h[:], wg[:, t, P * j0 : P * j1], ALU.mult)
+
+        pairs = {}
+
+        def round_page(t, c):
+            if t == 0:
+                pairs[c] = ring.tile([P, 2, CHUNK, 2], BF16, name=f"pairs{c}", tag="four_kib", bufs=4)
+            nc.scalar.copy(out=pairs[c][:, t // 2, :, t % 2], in_=page[t][:, CHUNK * c : CHUNK * (c + 1)])
+
+        def finish_page(t):
+            nc.sync.dma_start(out=out_rows[t], in_=page[t][:])
+            if t < PACK - 1:
+                for c in range(T2 // CHUNK):
+                    round_page(t, c)
+
+        woven = {}
+
+        def weave(c):
+            round_page(PACK - 1, c)
+            woven[c] = ring.tile([P, CHUNK * PACK], BF16, name=f"woven{c}", tag="woven", bufs=4, align_bytes=64)
+            words = pairs[c][:].rearrange("p u m e -> p (u m e)").bitcast(F32)
+            nc.scalar.copy(
+                out=woven[c][:].bitcast(F32).rearrange("p (m u) -> p m u", u=2),
+                in_=words.rearrange("p (u m) -> p m u", u=2),
+            )
+
+        def quantise_page(c):
+            cols = slice(CHUNK * c, CHUNK * (c + 1))
+            codes = ring.tile([P, CHUNK], U32, name="page_codes", bufs=4, align_bytes=64)
+            nc.vector.quantize_mx(out=codes[:].bitcast(FP8X4), scales=page_plane[:, cols], in_=woven[c][:])
+            nc.sync.dma_start(
+                out=out_2[0].rearrange("p m t -> p (m t)").bitcast(I32)[:, cols], in_=codes[:].bitcast(I32)
+            )
+
+        x_grouped = {}
+
+        def read_page(half):
+            x = x_all[:, half, :, :]
+            places = idx3[:, (XH // 16) * half : (XH // 16) * (half + 1)]
+            for t in range(PACK):
+                nc.vector.tensor_tensor(
+                    x[:, t, :], page[t][:].indirect(places), norm_sb[:, t, XH * half : XH * (half + 1)], ALU.subtract
+                )
+            x_grouped[half] = ring.tile([P, XH, PACK], BF16, name=f"x_grouped{half}", tag="w1_grouped", align_bytes=64)
+            nc.vector.tensor_copy(out=x_grouped[half][:], in_=x.rearrange("p t j -> p j t"))
+
+        def project(half):
+            x_codes = ring.tile([P, XH], U32, name="x_codes", align_bytes=64)
+            x_plane = ring.tile([P, XH], U8, name="x_plane", align_bytes=64)
+            nc.vector.quantize_mx(
+                out=x_codes[:].bitcast(FP8X4), scales=x_plane[:], in_=x_grouped[half][:].rearrange("p j t -> p (j t)")
+            )
+            for pair in range(2):
+                bank = psum.tile([P, 2, XH], F32, name="y_bank", tag="a", bufs=4)
+                for i in range(2):
+                    cols = slice(P * (2 * pair + i), P * (2 * pair + i + 1))
+                    nc.tensor.matmul_mx(
+                        out=bank[:, i, :],
+                        lhsT=w3_codes[:, cols].bitcast(FP8X4),
+                        lhsT_scale=w3_plane[:, cols],
+                        rhs=x_codes[:].bitcast(FP8X4),
+                        rhs_scale=x_plane[:],
+                        start=True,
+                        stop=True,
+                    )
+                y = ring.tile([P, 2, XH], F32, name="y", bufs=4)
+                nc.scalar.activation(y[:], bank[:], ACT.Abs)
+                rows = out_0.rearrange("(b p) j -> p b j", p=P)
+                nc.sync.dma_start(out=rows[:, 2 * pair : 2 * pair + 2, XH * half : XH * (half + 1)], in_=y[:])
+
+        def both_parts(j0):
+            cosine_part(j0)
+            cosine_part(j0 + 1)
+            sine_part(range(j0, j0 + 2))
+
+        for j in range(4):
+            cosine_part(j)
+        sine_part(range(0, 2))
+        put(0, 0, 2)
+        put(1, 0, 2)
+        sine_part(range(2, 4))
+        put(0, 2, 4)
+        put(1, 2, 4)
+        put(2, 0, 4)
+        both_parts(4)
+        put(0, 4, 6)
+        put(1, 4, 6)
+        both_parts(6)
+        put(0, 6, 8)
+        put(1, 6, 8)
+        put(2, 4, 8)
+        put(3, 0, 4)
+        put(3, 4, 8, tag="last", bufs=1)
+
+        w3_grouped = ring.tile([P, N, PACK], BF16, name="w3_grouped", tag="woven", bufs=4, align_bytes=64)
+        nc.scalar.copy(out=w3_grouped[:], in_=w3_raw[:].rearrange("p i n -> p n i"))
+        nc.vector.quantize_mx(
+            out=w3_codes[:].bitcast(FP8X4), scales=w3_plane[:], in_=w3_grouped[:].rearrange("p n i -> p (n i)")
+        )
+        for t in range(PACK):
+            finish_page(t)
+
+        nc.gpsimd.tensor_copy(clock[:, 8:9], page[3][:, 0:1])
+        x_all = ring.tile([P, 2, PACK, XH], F32, name="x_all", tag="last", bufs=1)
+        for c in range(T2 // CHUNK):
+            weave(c)
+        read_page(0)
+        project(0)
+        read_page(1)
+        project(1)
+        for c in range(T2 // CHUNK):
+            quantise_page(c)
+        for quad in range(4):
+            nc.sync.dma_start(
+                out=out_3[0, 4 * quad : 4 * quad + 4, :].bitcast(I32),
+                in_=page_plane[32 * quad : 32 * quad + 4, :].bitcast(I32),
+            )

@@ -52,17 +52,14 @@ def tile_list_head_impulse_page_kernel(
         w1_plane = keep.tile([P, PASSES, H], U8, name="w1_plane", align_bytes=64)
         g = keep.tile([P, PACK], F32, name="g")
         g_neg = keep.tile([P, PACK], F32, name="g_neg")
-        wg = keep.tile([P, PACK, S], F32, name="wg")
+        wg = keep.tile([P, PACK - 1, S], F32, name="wg")
+        wg_last = ring.tile([P, S], F32, name="wg_last", tag="wg_last", bufs=1, align_bytes=64)
         page = [keep.tile([P, T2], F32, name=f"page{t}") for t in range(PACK)]
         norm_sb = keep.tile([P, PACK, R], F32, name="norm_sb")
         w3_raw = keep.tile([P, PACK, N], F32, name="w3_raw")
-        w3_codes = keep.tile([P, N], U32, name="w3_codes", align_bytes=64)
         w3_plane = keep.tile([P, N], U8, name="w3_plane", align_bytes=64)
         ident = keep.tile([P, P], F32, name="ident")
-        clock = keep.tile([P, 16], F32, name="clock")
         warm = keep.tile([P, 1], F32, name="warm")
-        two_sq = [keep.tile([P, PACK, P], F32, name=f"two_sq{j}") for j in range(JB)]
-        neg_sin = [keep.tile([P, PACK, P], F32, name=f"neg_sin{j}") for j in range(JB)]
         page_plane = keep.tile([P, T2], U8, name="page_plane", align_bytes=64)
 
         page_rows = page0.rearrange("(p t) m -> t p m", t=PACK)
@@ -95,18 +92,18 @@ def tile_list_head_impulse_page_kernel(
                 out=w2_plane[32 * quad : 32 * quad + 4, :, :].bitcast(I32),
                 in_=w2_scales[:, 4 * quad : 4 * quad + 4, :].rearrange("a r c -> r a c").bitcast(I32),
             )
-        w1_raw = {}
-
-        def load_w1(a):
-            for c in range(2):
-                w1_raw[a, c] = ring.tile([P, PACK, H // 2], F32, name=f"w1_raw{a}{c}", tag="four_kib", bufs=4)
-                rows = w1[512 * a : 512 * (a + 1), (H // 2) * c : (H // 2) * (c + 1)]
-                nc.sync.dma_start(out=w1_raw[a, c][:], in_=rows.rearrange("(p i) c -> p i c", i=PACK))
-
         load_table(1)
-        load_w1(0)
-        load_w1(1)
-        first, second = slice(0, HALF), slice(HALF, S)
+        w1_rows = w1.rearrange("(a p i) c -> a p i c", p=P, i=PACK)
+        w1_first = keep.tile([P, PACK, H], F32, name="w1_first")
+        nc.sync.dma_start(out=w1_first[:], in_=w1_rows[0])
+        w1_raw = {}
+        for c in range(2):
+            cols = slice((H // 2) * c, (H // 2) * (c + 1))
+            w1_raw[0, c] = w1_first[:, :, cols]
+            piece = ring.tile([P, PACK, H // 2], F32, name=f"w1_second{c}", tag="four_kib", bufs=4, align_bytes=64)
+            nc.sync.dma_start(out=piece[:], in_=w1_rows[1][:, :, cols])
+            w1_raw[1, c] = piece[:]
+        second = slice(HALF, S)
         nc.sync.dma_start(idx2[:], offs2)
         nc.sync.dma_start(out=g[:], in_=gain.rearrange("(p t) -> p t", t=PACK))
         nc.sync.dma_start(out=page[0][:], in_=page_rows[0])
@@ -114,13 +111,14 @@ def tile_list_head_impulse_page_kernel(
         nc.sync.dma_start(out=page[1][:], in_=page_rows[1])
         load_wg(slice(0, 2), slice(QUARTER, HALF))
         nc.sync.dma_start(out=page[2][:], in_=page_rows[2])
-        load_wg(slice(2, 4), first)
-        load_wg(slice(0, 2), second)
+        load_wg(slice(2, 3), slice(0, HALF))
         nc.sync.dma_start(out=w3_raw[:], in_=w3.rearrange("(p i) n -> p i n", i=PACK))
-        load_wg(slice(2, 4), second)
-        nc.sync.dma_start(out=page[3][:], in_=page_rows[3])
+        load_wg(slice(0, 3), second)
         nc.sync.dma_start(idx3[:], offs3)
         nc.sync.dma_start(out=norm_sb[:], in_=norm.rearrange("(p t) j -> p t j", t=PACK))
+        nc.sync.dma_start(out=page[3][:], in_=page_rows[3])
+        for quad in range(4):
+            nc.sync.dma_start(out=wg_last[32 * quad : 32 * quad + 32, :], in_=wgs_rows[:, PACK - 1, :])
 
         nc.scalar.activation(warm[:], ident[:, 0:1], ACT.Sin)
 
@@ -140,11 +138,7 @@ def tile_list_head_impulse_page_kernel(
 
         def quantise_w1(a, c):
             grouped = ring.tile([P, H // 2, PACK], BF16, name="w1_grouped", tag="w1_grouped", align_bytes=64)
-            rows = w1_raw[a, c][:].rearrange("p i c -> p c i")
-            if (a, c) == (0, 0):
-                nc.scalar.copy(out=grouped[:], in_=rows)
-            else:
-                nc.vector.tensor_copy(out=grouped[:], in_=rows)
+            nc.vector.tensor_copy(out=grouped[:], in_=w1_raw[a, c].rearrange("p i c -> p c i"))
             cols = slice((H // 2) * c, (H // 2) * (c + 1))
             nc.vector.quantize_mx(
                 out=w1_codes[:, a, cols].bitcast(FP8X4),
@@ -157,7 +151,7 @@ def tile_list_head_impulse_page_kernel(
         for a in range(PASSES):
             for c in range(2):
                 quantise_w1(a, c)
-        nc.vector.tensor_scalar(g_neg[:], g[:], -1.0, None, ALU.mult)
+        nc.gpsimd.tensor_scalar(g_neg[:], g[:], -1.0, 0.0, ALU.mult, ALU.add)
 
         def table_pass(bank, j, a, codes, plane):
             cols = slice(P * j, P * (j + 1))
@@ -171,52 +165,67 @@ def tile_list_head_impulse_page_kernel(
                 stop=(a == PASSES - 1),
             )
 
+        parts = {}
+
         def cosine_part(j):
-            bank = psum.tile([P, H], F32, name="b_bank", tag="sum" if j < 4 else "a", bufs=4)
+            tag = "early" if j < JB // 2 else "four_kib"
+            parts[j] = ring.tile([P, 2, PACK, P], F32, name=f"parts{j}", tag=tag, bufs=4, align_bytes=64)
+            tag, bufs = ("four", 4) if j < JB // 2 else ("two_a", 2)
+            bank = psum.tile([P, H], F32, name="b_bank", tag=tag, bufs=bufs)
             for a in range(PASSES):
                 table_pass(bank, j, a, w2_codes[:, a, :].bitcast(FP4X4), w2_plane[:, a, :])
             half_sin = ring.tile([P, PACK, P], F32, name="half_sin")
             nc.scalar.activation(half_sin[:], bank[:].rearrange("p (q t) -> p t q", t=PACK), ACT.Sin, scale=0.5)
-            nc.scalar.activation(two_sq[j][:], half_sin[:], ACT.Square, scale=math.sqrt(2.0))
+            nc.scalar.activation(parts[j][:, 0, :, :], half_sin[:], ACT.Square, scale=math.sqrt(2.0))
 
         def sine_part(js):
-            banks = [psum.tile([P, H], F32, name=f"a_bank{j}", tag="a", bufs=4) for j in js]
+            tag = "two_a" if js[0] == 0 else "two_b"
+            banks = [psum.tile([P, H], F32, name=f"a_bank{j}", tag=tag, bufs=2) for j in js]
             for a in range(PASSES):
                 for bank, j in zip(banks, js):
                     table_pass(bank, j, a, w1_codes[:, a, :].bitcast(FP8X4), w1_plane[:, a, :])
             for bank, j in zip(banks, js):
                 nc.scalar.activation(
-                    neg_sin[j][:], bank[:].rearrange("p (q t) -> p t q", t=PACK), ACT.Sin, scale=-1.0
+                    parts[j][:, 1, :, :], bank[:].rearrange("p (q t) -> p t q", t=PACK), ACT.Sin, scale=-1.0
                 )
 
-        def put(t, j0, j1, tag="h", bufs=3):
-            width = P * (j1 - j0)
-            bank = psum.tile([P, width], F32, name="sum_bank", tag="sum", bufs=4)
+        def make_h(t, j0, j1, h):
+            tag, bufs = ("two_b", 2) if (j0, j1) == (0, 2) else ("four", 4)
+            bank = psum.tile([P, P * (j1 - j0)], F32, name="sum_bank", tag=tag, bufs=bufs)
             for j in range(j0, j1):
                 cols = slice(P * (j - j0), P * (j - j0 + 1))
                 nc.tensor.matmul(
-                    bank[:, cols], two_sq[j][:, t, :], ident[:], start=True, stop=False, is_transpose=True
+                    bank[:, cols], parts[j][:, 0, t, :], ident[:], start=True, stop=False, is_transpose=True
                 )
                 nc.tensor.matmul(
-                    bank[:, cols], neg_sin[j][:, t, :], ident[:], start=False, stop=True, is_transpose=True
+                    bank[:, cols], parts[j][:, 1, t, :], ident[:], start=False, stop=True, is_transpose=True
                 )
-            h = ring.tile([P, width], F32, name="h", tag=tag, bufs=bufs)
-            nc.scalar.activation(h[:], bank[:], ACT.Identity, bias=g[:, t : t + 1], scale=g_neg[:, t : t + 1])
-            if t == 0 and j0 == 0:
-                nc.gpsimd.tensor_copy(clock[:, 0:1], h[:, 0:1])
+            nc.scalar.activation(h, bank[:], ACT.Identity, bias=g[:, t : t + 1], scale=g_neg[:, t : t + 1])
+
+        def put(t, j0, j1):
+            h = keep.tile([P, P * (j1 - j0)], F32, name=f"h{t}{j0}")
+            make_h(t, j0, j1, h[:])
             places = idx2[:, (P // 16) * j0 : (P // 16) * j1]
             nc.vector.tensor_tensor(page[t][:].indirect(places), h[:], wg[:, t, P * j0 : P * j1], ALU.mult)
+
+        def put_last():
+            h = ring.tile([P, S], F32, name="h_last", tag="x0", bufs=1)
+            make_h(PACK - 1, 0, JB // 2, h[:, 0:HALF])
+            make_h(PACK - 1, JB // 2, JB, h[:, HALF:S])
+            nc.vector.tensor_tensor(page[PACK - 1][:].indirect(idx2[:]), h[:], wg_last[:], ALU.mult)
 
         pairs = {}
 
         def round_page(t, c):
             if t == 0:
-                pairs[c] = ring.tile([P, 2, CHUNK, 2], BF16, name=f"pairs{c}", tag="four_kib", bufs=4)
+                pairs[c] = ring.tile([P, 2, CHUNK, 2], BF16, name=f"pairs{c}", tag="four_kib", bufs=4, align_bytes=64)
             nc.scalar.copy(out=pairs[c][:, t // 2, :, t % 2], in_=page[t][:, CHUNK * c : CHUNK * (c + 1)])
 
         def finish_page(t):
-            nc.sync.dma_start(out=out_rows[t], in_=page[t][:])
-            if t < PACK - 1:
+            if t == PACK - 1:
+                nc.sync.dma_start(out=out_rows[t], in_=page[t][:])
+            else:
+                nc.gpsimd.dma_start(out=out_rows[t], in_=page[t][:])
                 for c in range(T2 // CHUNK):
                     round_page(t, c)
 
@@ -242,14 +251,14 @@ def tile_list_head_impulse_page_kernel(
         x_grouped = {}
 
         def read_page(half):
-            x = x_all[:, half, :, :]
+            x = ring.tile([P, PACK, XH], F32, name=f"x{half}", tag="x0", bufs=1)
             places = idx3[:, (XH // 16) * half : (XH // 16) * (half + 1)]
             for t in range(PACK):
                 nc.vector.tensor_tensor(
                     x[:, t, :], page[t][:].indirect(places), norm_sb[:, t, XH * half : XH * (half + 1)], ALU.subtract
                 )
             x_grouped[half] = ring.tile([P, XH, PACK], BF16, name=f"x_grouped{half}", tag="w1_grouped", align_bytes=64)
-            nc.vector.tensor_copy(out=x_grouped[half][:], in_=x.rearrange("p t j -> p j t"))
+            nc.vector.tensor_copy(out=x_grouped[half][:], in_=x[:].rearrange("p t j -> p j t"))
 
         def project(half):
             x_codes = ring.tile([P, XH], U32, name="x_codes", align_bytes=64)
@@ -258,7 +267,7 @@ def tile_list_head_impulse_page_kernel(
                 out=x_codes[:].bitcast(FP8X4), scales=x_plane[:], in_=x_grouped[half][:].rearrange("p j t -> p (j t)")
             )
             for pair in range(2):
-                bank = psum.tile([P, 2, XH], F32, name="y_bank", tag="a", bufs=4)
+                bank = psum.tile([P, 2, XH], F32, name="y_bank", tag="four", bufs=4)
                 for i in range(2):
                     cols = slice(P * (2 * pair + i), P * (2 * pair + i + 1))
                     nc.tensor.matmul_mx(
@@ -296,10 +305,10 @@ def tile_list_head_impulse_page_kernel(
         put(0, 6, 8)
         put(1, 6, 8)
         put(2, 4, 8)
-        put(3, 0, 4)
-        put(3, 4, 8, tag="last", bufs=1)
+        put_last()
 
-        w3_grouped = ring.tile([P, N, PACK], BF16, name="w3_grouped", tag="woven", bufs=4, align_bytes=64)
+        w3_codes = ring.tile([P, N], U32, name="w3_codes", tag="wg_last", bufs=1, align_bytes=64)
+        w3_grouped = ring.tile([P, N, PACK], BF16, name="w3_grouped", tag="early", bufs=4, align_bytes=64)
         nc.scalar.copy(out=w3_grouped[:], in_=w3_raw[:].rearrange("p i n -> p n i"))
         nc.vector.quantize_mx(
             out=w3_codes[:].bitcast(FP8X4), scales=w3_plane[:], in_=w3_grouped[:].rearrange("p n i -> p (n i)")
@@ -307,8 +316,6 @@ def tile_list_head_impulse_page_kernel(
         for t in range(PACK):
             finish_page(t)
 
-        nc.gpsimd.tensor_copy(clock[:, 8:9], page[3][:, 0:1])
-        x_all = ring.tile([P, 2, PACK, XH], F32, name="x_all", tag="last", bufs=1)
         for c in range(T2 // CHUNK):
             weave(c)
         read_page(0)

import math
from contextlib import ExitStack

import concourse.mybir as mybir
from concourse.masks import make_identity

K, H, N, T, S, T2, R = 1024, 512, 512, 4096, 1024, 2048, 512
FLOPS = 2 * (2 * K * H * S + H * N * R)

F32 = mybir.dt.float32
BF16 = mybir.dt.bfloat16
I32 = mybir.dt.int32
U32 = mybir.dt.uint32
U16 = mybir.dt.uint16
U8 = mybir.dt.uint8
FP8X4 = mybir.dt.float8_e4m3fn_x4
FP4X4 = mybir.dt.float4_e2m1fn_x4
ACT = mybir.ActivationFunctionType
ALU = mybir.AluOpType

P = 128
PACK = 4
PASSES = K // (P * PACK)
JB = S // P
HALF = S // 2
QUARTER = S // 4
CHUNK = 512
XH = R // 2


def tile_list_head_impulse_page_kernel(
    tc, tab_words, tab_scales, offs, offs2, offs3, w1, w2_words, w2_scales, gain, wgs, page0, norm, w3,
    out_0, out_1, out_2, out_3,
):
    nc = tc.nc
    with ExitStack() as ctx:
        keep = ctx.enter_context(tc.tile_pool(name="keep", bufs=1))
        ring = ctx.enter_context(tc.tile_pool(name="ring", bufs=2))
        psum = ctx.enter_context(tc.psum_pool(name="psum", bufs=2))

        idx = keep.tile([P, S // 16], U16, name="idx")
        idx2 = keep.tile([P, S // 16], U16, name="idx2")
        idx3 = keep.tile([P, R // 16], U16, name="idx3")
        tab = [keep.tile([P, T], U32, name=f"tab{a}") for a in range(PASSES)]
        tab_rows = keep.tile([P, T], U8, name="tab_rows")
        picked_rows = keep.tile([P, S], U8, name="picked_rows")
        v_scales = keep.tile([P, PASSES, S], U8, name="v_scales", align_bytes=64)
        v_words = [keep.tile([P, S], U32, name=f"v_words{a}", align_bytes=64) for a in range(PASSES)]
        w2_codes = keep.tile([P, PASSES, 2 * H], U8, name="w2_codes", align_bytes=64)
        w2_plane = keep.tile([P, PASSES, H], U8, name="w2_plane", align_bytes=64)
        w1_codes = keep.tile([P, PASSES, H], U32, name="w1_codes", align_bytes=64)
        w1_plane = keep.tile([P, PASSES, H], U8, name="w1_plane", align_bytes=64)
        g = keep.tile([P, PACK], F32, name="g")
        g_neg = keep.tile([P, PACK], F32, name="g_neg")
        wg = keep.tile([P, PACK - 1, S], F32, name="wg")
        wg_last = ring.tile([P, S], F32, name="wg_last", tag="wg_last", bufs=1, align_bytes=64)
        page = [keep.tile([P, T2], F32, name=f"page{t}") for t in range(PACK)]
        norm_sb = keep.tile([P, PACK, R], F32, name="norm_sb")
        w3_raw = keep.tile([P, PACK, N], F32, name="w3_raw")
        w3_plane = keep.tile([P, N], U8, name="w3_plane", align_bytes=64)
        ident = keep.tile([P, P], F32, name="ident")
        warm = keep.tile([P, 1], F32, name="warm")
        page_plane = keep.tile([P, T2], U8, name="page_plane", align_bytes=64)

        page_rows = page0.rearrange("(p t) m -> t p m", t=PACK)
        out_rows = out_1.rearrange("(p t) m -> t p m", t=PACK)
        wgs_rows = wgs.rearrange("(q t) j -> q t j", t=PACK)

        def load_wg(ts, js):
            for quad in range(4):
                nc.sync.dma_start(out=wg[32 * quad : 32 * quad + 32, ts, js], in_=wgs_rows[:, ts, js])

        def load_table(a):
            nc.sync.dma_start(
                out=tab[a][:].bitcast(I32), in_=tab_words[a].rearrange("p t i -> p (t i)").bitcast(I32)
            )

        nc.vector.memset(tab_rows[32:64, :].bitcast(I32), 0)
        nc.vector.memset(tab_rows[64:128, :].bitcast(I32), 0)
        nc.vector.memset(w2_plane[:].rearrange("p a t -> p (a t)").bitcast(I32), 0)
        nc.vector.memset(v_scales[:].rearrange("p a t -> p (a t)").bitcast(I32), 0)
        make_identity(nc, ident[:])

        nc.sync.dma_start(idx[:], offs)
        nc.sync.dma_start(
            out=tab_rows[0:32, :].bitcast(I32), in_=tab_scales.rearrange("a q t -> q a t").bitcast(I32)
        )
        load_table(0)
        nc.sync.dma_start(out=w2_codes[:].bitcast(I32), in_=w2_words.rearrange("a p c -> p a c").bitcast(I32))
        for quad in range(4):
            nc.scalar.dma_start(
                out=w2_plane[32 * quad : 32 * quad + 4, :, :].bitcast(I32),
                in_=w2_scales[:, 4 * quad : 4 * quad + 4, :].rearrange("a r c -> r a c").bitcast(I32),
            )
        load_table(1)
        w1_rows = w1.rearrange("(a p i) c -> a p i c", p=P, i=PACK)
        w1_first = keep.tile([P, PACK, H], F32, name="w1_first")
        nc.sync.dma_start(out=w1_first[:], in_=w1_rows[0])
        w1_raw = {}
        for c in range(2):
            cols = slice((H // 2) * c, (H // 2) * (c + 1))
            w1_raw[0, c] = w1_first[:, :, cols]
            piece = ring.tile([P, PACK, H // 2], F32, name=f"w1_second{c}", tag="four_kib", bufs=4, align_bytes=64)
            nc.sync.dma_start(out=piece[:], in_=w1_rows[1][:, :, cols])
            w1_raw[1, c] = piece[:]
        second = slice(HALF, S)
        nc.sync.dma_start(idx2[:], offs2)
        nc.sync.dma_start(out=g[:], in_=gain.rearrange("(p t) -> p t", t=PACK))
        nc.sync.dma_start(out=page[0][:], in_=page_rows[0])
        load_wg(slice(0, 2), slice(0, QUARTER))
        nc.sync.dma_start(out=page[1][:], in_=page_rows[1])
        load_wg(slice(0, 2), slice(QUARTER, HALF))
        nc.sync.dma_start(out=page[2][:], in_=page_rows[2])
        load_wg(slice(2, 3), slice(0, HALF))
        nc.sync.dma_start(out=w3_raw[:], in_=w3.rearrange("(p i) n -> p i n", i=PACK))
        load_wg(slice(0, 3), second)
        nc.sync.dma_start(idx3[:], offs3)
        nc.sync.dma_start(out=norm_sb[:], in_=norm.rearrange("(p t) j -> p t j", t=PACK))
        nc.sync.dma_start(out=page[3][:], in_=page_rows[3])
        for quad in range(4):
            nc.sync.dma_start(out=wg_last[32 * quad : 32 * quad + 32, :], in_=wgs_rows[:, PACK - 1, :])

        nc.scalar.activation(warm[:], ident[:, 0:1], ACT.Sin)

        nc.vector.tensor_copy(picked_rows[:], tab_rows[:].indirect(idx[:]))
        for quad in range(4):
            nc.scalar.dma_start(
                out=v_scales[32 * quad : 32 * quad + 4, :, :].bitcast(I32),
                in_=picked_rows[8 * quad : 8 * quad + 8, :].bitcast(I32),
            )
        nc.vector.tensor_copy(v_words[0][:], tab[0][:].indirect(idx[:]))

        def pick_second_pass(half):
            cols = slice(HALF * half, HALF * (half + 1))
            nc.vector.tensor_copy(
                v_words[1][:, cols], tab[1][:].indirect(idx[:, (HALF // 16) * half : (HALF // 16) * (half + 1)])
            )

        def quantise_w1(a, c):
            grouped = ring.tile([P, H // 2, PACK], BF16, name="w1_grouped", tag="w1_grouped", align_bytes=64)
            nc.vector.tensor_copy(out=grouped[:], in_=w1_raw[a, c].rearrange("p i c -> p c i"))
            cols = slice((H // 2) * c, (H // 2) * (c + 1))
            nc.vector.quantize_mx(
                out=w1_codes[:, a, cols].bitcast(FP8X4),
                scales=w1_plane[:, a, cols],
                in_=grouped[:].rearrange("p c i -> p (c i)"),
            )

        pick_second_pass(0)
        pick_second_pass(1)
        for a in range(PASSES):
            for c in range(2):
                quantise_w1(a, c)
        nc.gpsimd.tensor_scalar(g_neg[:], g[:], -1.0, 0.0, ALU.mult, ALU.add)

        def table_pass(bank, j, a, codes, plane):
            cols = slice(P * j, P * (j + 1))
            nc.tensor.matmul_mx(
                out=bank[:],
                lhsT=v_words[a][:, cols].bitcast(FP8X4),
                lhsT_scale=v_scales[:, a, cols],
                rhs=codes,
                rhs_scale=plane,
                start=(a == 0),
                stop=(a == PASSES - 1),
            )

        parts = {}

        def cosine_part(j):
            tag = "early" if j < JB // 2 else "four_kib"
            parts[j] = ring.tile([P, 2, PACK, P], F32, name=f"parts{j}", tag=tag, bufs=4, align_bytes=64)
            tag, bufs = ("four", 4) if j < JB // 2 else ("two_a", 2)
            bank = psum.tile([P, H], F32, name="b_bank", tag=tag, bufs=bufs)
            for a in range(PASSES):
                table_pass(bank, j, a, w2_codes[:, a, :].bitcast(FP4X4), w2_plane[:, a, :])
            half_sin = ring.tile([P, PACK, P], F32, name="half_sin")
            nc.scalar.activation(half_sin[:], bank[:].rearrange("p (q t) -> p t q", t=PACK), ACT.Sin, scale=0.5)
            nc.scalar.activation(parts[j][:, 0, :, :], half_sin[:], ACT.Square, scale=math.sqrt(2.0))

        def sine_part(js):
            tag = "two_a" if js[0] == 0 else "two_b"
            banks = [psum.tile([P, H], F32, name=f"a_bank{j}", tag=tag, bufs=2) for j in js]
            for a in range(PASSES):
                for bank, j in zip(banks, js):
                    table_pass(bank, j, a, w1_codes[:, a, :].bitcast(FP8X4), w1_plane[:, a, :])
            for bank, j in zip(banks, js):
                nc.scalar.activation(
                    parts[j][:, 1, :, :], bank[:].rearrange("p (q t) -> p t q", t=PACK), ACT.Sin, scale=-1.0
                )

        def make_h(t, j0, j1, h):
            tag, bufs = ("two_b", 2) if (j0, j1) == (0, 2) else ("four", 4)
            bank = psum.tile([P, P * (j1 - j0)], F32, name="sum_bank", tag=tag, bufs=bufs)
            for j in range(j0, j1):
                cols = slice(P * (j - j0), P * (j - j0 + 1))
                nc.tensor.matmul(
                    bank[:, cols], parts[j][:, 0, t, :], ident[:], start=True, stop=False, is_transpose=True
                )
                nc.tensor.matmul(
                    bank[:, cols], parts[j][:, 1, t, :], ident[:], start=False, stop=True, is_transpose=True
                )
            nc.scalar.activation(h, bank[:], ACT.Identity, bias=g[:, t : t + 1], scale=g_neg[:, t : t + 1])

        def put(t, j0, j1):
            h = keep.tile([P, P * (j1 - j0)], F32, name=f"h{t}{j0}")
            make_h(t, j0, j1, h[:])
            places = idx2[:, (P // 16) * j0 : (P // 16) * j1]
            nc.vector.tensor_tensor(page[t][:].indirect(places), h[:], wg[:, t, P * j0 : P * j1], ALU.mult)

        def put_last():
            h = ring.tile([P, S], F32, name="h_last", tag="x0", bufs=1)
            make_h(PACK - 1, 0, JB // 2, h[:, 0:HALF])
            make_h(PACK - 1, JB // 2, JB, h[:, HALF:S])
            nc.vector.tensor_tensor(page[PACK - 1][:].indirect(idx2[:]), h[:], wg_last[:], ALU.mult)

        pairs = {}

        def round_page(t, c):
            if t == 0:
                pairs[c] = ring.tile([P, 2, CHUNK, 2], BF16, name=f"pairs{c}", tag="four_kib", bufs=4, align_bytes=64)
            nc.scalar.copy(out=pairs[c][:, t // 2, :, t % 2], in_=page[t][:, CHUNK * c : CHUNK * (c + 1)])

        def finish_page(t):
            if t == PACK - 1:
                nc.sync.dma_start(out=out_rows[t], in_=page[t][:])
            else:
                nc.gpsimd.dma_start(out=out_rows[t], in_=page[t][:])
                for c in range(T2 // CHUNK):
                    round_page(t, c)

        woven = {}

        def weave(c):
            round_page(PACK - 1, c)
            woven[c] = ring.tile([P, CHUNK * PACK], BF16, name=f"woven{c}", tag="woven", bufs=4, align_bytes=64)
            words = pairs[c][:].rearrange("p u m e -> p (u m e)").bitcast(F32)
            nc.scalar.copy(
                out=woven[c][:].bitcast(F32).rearrange("p (m u) -> p m u", u=2),
                in_=words.rearrange("p (u m) -> p m u", u=2),
            )

        def quantise_page(c):
            cols = slice(CHUNK * c, CHUNK * (c + 1))
            codes = ring.tile([P, CHUNK], U32, name="page_codes", bufs=4, align_bytes=64)
            nc.vector.quantize_mx(out=codes[:].bitcast(FP8X4), scales=page_plane[:, cols], in_=woven[c][:])
            nc.sync.dma_start(
                out=out_2[0].rearrange("p m t -> p (m t)").bitcast(I32)[:, cols], in_=codes[:].bitcast(I32)
            )

        x_grouped = {}

        def read_page(half):
            x = ring.tile([P, PACK, XH], F32, name=f"x{half}", tag="x0", bufs=1)
            places = idx3[:, (XH // 16) * half : (XH // 16) * (half + 1)]
            for t in range(PACK):
                nc.vector.tensor_tensor(
                    x[:, t, :], page[t][:].indirect(places), norm_sb[:, t, XH * half : XH * (half + 1)], ALU.subtract
                )
            x_grouped[half] = ring.tile([P, XH, PACK], BF16, name=f"x_grouped{half}", tag="w1_grouped", align_bytes=64)
            nc.vector.tensor_copy(out=x_grouped[half][:], in_=x[:].rearrange("p t j -> p j t"))

        def project(half):
            x_codes = ring.tile([P, XH], U32, name="x_codes", align_bytes=64)
            x_plane = ring.tile([P, XH], U8, name="x_plane", align_bytes=64)
            nc.vector.quantize_mx(
                out=x_codes[:].bitcast(FP8X4), scales=x_plane[:], in_=x_grouped[half][:].rearrange("p j t -> p (j t)")
            )
            for pair in range(2):
                bank = psum.tile([P, 2, XH], F32, name="y_bank", tag="four", bufs=4)
                for i in range(2):
                    cols = slice(P * (2 * pair + i), P * (2 * pair + i + 1))
                    nc.tensor.matmul_mx(
                        out=bank[:, i, :],
                        lhsT=w3_codes[:, cols].bitcast(FP8X4),
                        lhsT_scale=w3_plane[:, cols],
                        rhs=x_codes[:].bitcast(FP8X4),
                        rhs_scale=x_plane[:],
                        start=True,
                        stop=True,
                    )
                y = ring.tile([P, 2, XH], F32, name="y", bufs=4)
                nc.scalar.activation(y[:], bank[:], ACT.Abs)
                rows = out_0.rearrange("(b p) j -> p b j", p=P)
                nc.sync.dma_start(out=rows[:, 2 * pair : 2 * pair + 2, XH * half : XH * (half + 1)], in_=y[:])

        def both_parts(j0):
            cosine_part(j0)
            cosine_part(j0 + 1)
            sine_part(range(j0, j0 + 2))

        for j in range(4):
            cosine_part(j)
        sine_part(range(0, 2))
        put(0, 0, 2)
        put(1, 0, 2)
        sine_part(range(2, 4))
        put(0, 2, 4)
        put(1, 2, 4)
        put(2, 0, 4)
        both_parts(4)
        put(0, 4, 6)
        put(1, 4, 6)
        both_parts(6)
        put(0, 6, 8)
        put(1, 6, 8)
        put(2, 4, 8)
        put_last()

        w3_codes = ring.tile([P, N], U32, name="w3_codes", tag="wg_last", bufs=1, align_bytes=64)
        w3_grouped = ring.tile([P, N, PACK], BF16, name="w3_grouped", tag="early", bufs=4, align_bytes=64)
        nc.scalar.copy(out=w3_grouped[:], in_=w3_raw[:].rearrange("p i n -> p n i"))
        nc.vector.quantize_mx(
            out=w3_codes[:].bitcast(FP8X4), scales=w3_plane[:], in_=w3_grouped[:].rearrange("p n i -> p (n i)")
        )
        for t in range(PACK):
            finish_page(t)

        for c in range(T2 // CHUNK):
            weave(c)
        read_page(0)
        project(0)
        read_page(1)
        project(1)
        for c in range(T2 // CHUNK):
            quantise_page(c)
        for quad in range(4):
            nc.sync.dma_start(
                out=out_3[0, 4 * quad : 4 * quad + 4, :].bitcast(I32),
                in_=page_plane[32 * quad : 32 * quad + 4, :].bitcast(I32),
            )
